import numpy as np
import ml_dtypes


def mxq(x, axis, fmt="e4m3"):
    dtype, down = {"e4m3": (ml_dtypes.float8_e4m3fn, 7), "e5m2": (ml_dtypes.float8_e5m2, 14)}[fmt]
    v = np.moveaxis(np.asarray(x, np.float32).astype(ml_dtypes.bfloat16).astype(np.float64), axis, -1)
    blocks = v.reshape(v.shape[:-1] + (-1, 32))
    amax = np.abs(blocks).max(-1, keepdims=True)
    byte = np.maximum(np.where(amax > 0, np.frexp(amax)[1] - 1 + 127, 0) - down, 1)
    scale = np.exp2(byte - 127.0)
    codes = (blocks / scale).astype(np.float32).astype(dtype).astype(np.float64)
    return np.moveaxis((codes * scale).reshape(v.shape), -1, axis)


WIDE = False


def mx_kscale(k):
    if not WIDE:
        return np.ones(k)
    levels = np.array([10, -10, 5, -5, 0])
    if k % 512:
        return np.exp2(np.random.permutation(np.resize(levels, k // 32))).repeat(32)
    a = np.empty((k // 512, 16))
    for p in range(k // 512):
        a[p, :8] = np.random.permutation(np.resize(levels, 8))
        for g in range(8):
            far = levels[np.abs(levels - a[p, g]) >= 10]
            a[p, g + 8] = far[np.random.randint(len(far))]
    return np.exp2(a.ravel()).repeat(32)


def f64(x):
    return np.asarray(x).astype(np.float64)


def striped(idx):
    return np.tile(idx.reshape(-1, 16).T, (8, 1)).astype(np.uint16)


def unstriped(offs):
    return offs[:16].T.reshape(-1).astype(np.int64)


E2M1 = np.array([0.0, 0.5, 1.0, 1.5, 2.0, 3.0, 4.0, 6.0, -0.0, -0.5, -1.0, -1.5, -2.0, -3.0, -4.0, -6.0])


def pack_weight(w, fmt):
    k, n = w.shape
    w = f64(np.asarray(w, np.float32).astype(ml_dtypes.bfloat16)).reshape(k // 32, 32, n)
    amax = np.abs(w).max(1)
    if fmt == "e4m3":
        byte = np.frexp(amax)[1] - 1 + 127 - 7
    else:
        mant, ex = np.frexp(amax / 6.0)
        byte = np.where(mant > 0.5, ex, ex - 1) + 127
    byte = np.clip(np.where(amax > 0, byte, 1), 1, 254)
    scaled = (w * np.exp2(127.0 - byte)[:, None, :]).reshape(k, n).astype(np.float32)
    by_word = np.ascontiguousarray(scaled.reshape(k // 512, 128, 4, n).transpose(0, 1, 3, 2))
    if fmt == "e4m3":
        words = by_word.astype(ml_dtypes.float8_e4m3fn).view(np.uint8)
    else:
        c = by_word.astype(ml_dtypes.float4_e2m1fn).view(np.uint8) & 0xF
        words = (c[..., 0::2] | (c[..., 1::2] << 4)).reshape(k // 512, 128, 2 * n)
    return np.ascontiguousarray(words), np.ascontiguousarray(byte.astype(np.uint8).reshape(k // 512, 16, n))


def unpack_weight(words, scales, fmt):
    g, _, n = scales.shape
    words = np.ascontiguousarray(words).reshape(g, 128, n, -1)
    if fmt == "e4m3":
        vals = words.view(ml_dtypes.float8_e4m3fn).astype(np.float64)
    else:
        nib = np.empty((g, 128, n, 4), np.uint8)
        nib[..., 0::2] = words & 0xF
        nib[..., 1::2] = words >> 4
        vals = E2M1[nib]
    vals = vals * np.repeat(np.exp2(scales.astype(np.float64) - 127.0), 8, axis=1)[..., None]
    return vals.transpose(0, 1, 3, 2).reshape(g * 512, n)


def gelu(v):
    return 0.5 * v * (1.0 + np.tanh(np.sqrt(2.0 / np.pi) * (v + 0.044715 * v**3)))


K, T, S, H, N, K2, T2, P = 1536, 4096, 1024, 1024, 384, 512, 1024, 512


def setup_inputs():
    n = np.random.standard_normal
    s = mx_kscale(K)[:, None]
    s2 = mx_kscale(K2)[:, None]
    u = mx_kscale(H)[:, None]
    tab_words, tab_scales = pack_weight(n((K, T)) * s, "e4m3")
    tab2_words, tab2_scales = pack_weight(n((K2, T2)) * s2, "e4m3")
    w2_words, w2_scales = pack_weight(1.6 * n((H, N)) / np.sqrt(H) / u, "e2m1")
    return {
        "tab_words": tab_words, "tab_scales": tab_scales,
        "tab2_words": tab2_words, "tab2_scales": tab2_scales,
        "offs": striped(np.random.permutation(T)[:S]),
        "offs2": striped(np.random.permutation(T2)[:P]),
        "pos1": striped(np.random.permutation(S)[:P]),
        "w1": (0.42 * n((K, H)) / np.sqrt(K) / s).astype(np.float32),
        "phase": np.random.uniform(-0.8, 0.8, H).astype(np.float32),
        "gain": (np.exp(0.3 * n(H)) * u[:, 0]).astype(np.float32),
        "w2_words": w2_words, "w2_scales": w2_scales,
        "w3": (n((K2, N)) / np.sqrt(K2) / s2).astype(np.float32),
    }


def reference(tab_words, tab_scales, tab2_words, tab2_scales, offs, offs2, pos1,
              w1, phase, gain, w2_words, w2_scales, w3):
    v = unpack_weight(tab_words, tab_scales, "e4m3")[:, unstriped(offs)]
    v2 = unpack_weight(tab2_words, tab2_scales, "e4m3")[:, unstriped(offs2)]
    w2 = unpack_weight(w2_words, w2_scales, "e2m1")
    p = mxq(f64(w1), 0, "e4m3").T @ v
    h = f64(gain)[:, None] * np.sin(p + f64(phase)[:, None])
    y = w2.T @ mxq(h, 0, "e4m3")
    b = mxq(f64(w3), 0, "e4m3").T @ v2
    ys = y[:, unstriped(pos1)]
    return ys * b + np.maximum(ys, b)

@@ -1,0 +1,305 @@
+import math
+from contextlib import ExitStack
+
+import concourse.mybir as mybir
+
+K, T, S, H, N, K2, T2, PICK = 1536, 4096, 1024, 1024, 384, 512, 1024, 512
+FLOPS = 2 * K * H * S + 2 * H * N * S + 2 * K2 * N * PICK
+
+F32 = mybir.dt.float32
+BF16 = mybir.dt.bfloat16
+I32 = mybir.dt.int32
+U32 = mybir.dt.uint32
+U16 = mybir.dt.uint16
+U8 = mybir.dt.uint8
+FP8X4 = mybir.dt.float8_e4m3fn_x4
+FP4X4 = mybir.dt.float4_e2m1fn_x4
+ACT = mybir.ActivationFunctionType
+ALU = mybir.AluOpType
+
+P = 128
+PACK = 4
+KP = P * PACK
+PASSES = K // KP
+BLOCKS = H // KP
+NT = N // P
+HALF = 512
+CHUNKS = [(0, 0, 512, 256), (0, 512, 512, 256), (1, 0, 512, 256), (1, 512, 256, 256), (1, 768, 256, 128)]
+SPLIT_M = 48
+
+
+def tile_list_site_restocking_score_kernel(
+    tc, tab_words, tab_scales, tab2_words, tab2_scales, offs, offs2, pos1,
+    w1, phase, gain, w2_words, w2_scales, w3, out,
+):
+    nc = tc.nc
+    with ExitStack() as ctx:
+        keep = ctx.enter_context(tc.tile_pool(name="keep", bufs=1))
+        ring = ctx.enter_context(tc.tile_pool(name="ring", bufs=2))
+        psum = ctx.enter_context(tc.psum_pool(name="psum", bufs=1))
+
+        offs_t = keep.tile([P, S // 16], U16, name="offs_t")
+        offs2_t = keep.tile([P, PICK // 16], U16, name="offs2_t")
+        pos_t = keep.tile([P, PICK // 16], U16, name="pos_t")
+
+        tab_w = [keep.tile([P, T], I32, name=f"tab_w{a}", align_bytes=64) for a in range(PASSES)]
+        tab_s = keep.tile([P, T], U8, name="tab_s", align_bytes=64)
+        v_w = {}
+        v_s = keep.tile([P, S], U8, name="v_s", align_bytes=64)
+        tab2_s = keep.tile([P, T2], U8, name="tab2_s", align_bytes=64)
+        v2_w = keep.tile([P, PICK], U32, name="v2_w", align_bytes=64)
+        w2_w = keep.tile([P, BLOCKS, 2 * N], U8, name="w2_w", align_bytes=64)
+        w2_s = keep.tile([P, BLOCKS, N], U8, name="w2_s", align_bytes=64)
+
+        w1_raw, w1_w, w1_s = {}, {}, {}
+        for b in range(BLOCKS):
+            for a in range(PASSES):
+                w1_w[a, b] = keep.tile([P, KP], U32, name=f"w1_w{a}{b}", align_bytes=64)
+                w1_s[a, b] = keep.tile([P, KP], U8, name=f"w1_s{a}{b}", align_bytes=64)
+        w3_w = keep.tile([P, N], U32, name="w3_w", align_bytes=64)
+        w3_s = keep.tile([P, N], U8, name="w3_s", align_bytes=64)
+        phase_t = keep.tile([P, BLOCKS, PACK], F32, name="phase_t")
+        gain_t = keep.tile([P, BLOCKS, PACK], F32, name="gain_t")
+        bias_t = keep.tile([P, BLOCKS, PACK], F32, name="bias_t")
+        gain2_t = keep.tile([P, BLOCKS, PACK], F32, name="gain2_t")
+        h_w = [keep.tile([P, S], U32, name=f"h_w{b}", align_bytes=64) for b in range(BLOCKS)]
+        h_s = [keep.tile([P, S], U8, name=f"h_s{b}", align_bytes=64) for b in range(BLOCKS)]
+        y_t = [keep.tile([P, S], F32, name=f"y_t{n}", align_bytes=64) for n in range(NT)]
+
+        def staged(shape, dtype, name):
+            return ring.tile(shape, dtype, name=name, tag="staged", bufs=4, align_bytes=64)
+
+        def slot(i, shape, dtype, name):
+            return ring.tile(shape, dtype, name=name, tag=f"slot{i}", bufs=1, align_bytes=64)
+
+        def load_tab(a):
+            nc.sync.dma_start(out=tab_w[a][:], in_=tab_words[a].rearrange("p t i -> p (t i)").bitcast(I32))
+
+        def load_w1(a, b):
+            w1_raw[a, b] = staged([P, PACK, KP], F32, f"w1_raw{a}{b}")
+            rows = w1[a * KP : (a + 1) * KP, b * KP : (b + 1) * KP]
+            nc.sync.dma_start(out=w1_raw[a, b][:], in_=rows.rearrange("(p j) c -> p j c", j=PACK))
+
+        nc.vector.memset(tab_s[:].bitcast(I32), 0)
+        nc.vector.memset(tab2_s[:].bitcast(I32), 0)
+        nc.vector.memset(w2_s[:].bitcast(I32), 0)
+        load_tab(0)
+        for q in range(4):
+            nc.sync.dma_start(
+                out=tab_s[32 * q : 32 * q + 4 * PASSES, :].bitcast(I32),
+                in_=tab_scales[:, 4 * q : 4 * q + 4, :].bitcast(I32),
+            )
+        nc.sync.dma_start(out=offs_t[:], in_=offs)
+        nc.sync.dma_start(out=phase_t[:], in_=phase.rearrange("(b p t) -> p b t", p=P, t=PACK))
+        nc.sync.dma_start(out=gain_t[:], in_=gain.rearrange("(b p t) -> p b t", p=P, t=PACK))
+        nc.sync.dma_start(out=offs2_t[:], in_=offs2)
+        nc.sync.dma_start(out=pos_t[:], in_=pos1)
+        nc.sync.dma_start(out=w2_w[:].bitcast(I32), in_=w2_words.rearrange("a p c -> p a c").bitcast(I32))
+        load_w1(0, 0)
+        for a in range(1, PASSES):
+            load_tab(a)
+            load_w1(a, 0)
+        for q in range(4):
+            nc.gpsimd.dma_start(
+                out=tab2_s[32 * q : 32 * q + 4, :].bitcast(I32),
+                in_=tab2_scales[0, 4 * q : 4 * q + 4, :].bitcast(I32),
+            )
+        for q in range(4):
+            nc.gpsimd.dma_start(
+                out=w2_s[32 * q : 32 * q + 4, :, :].bitcast(I32),
+                in_=w2_scales[:, 4 * q : 4 * q + 4, :].rearrange("a r n -> r a n").bitcast(I32),
+            )
+        load_w1(0, 1)
+
+        nc.vector.tensor_scalar(bias_t[:], phase_t[:], -0.5, math.pi / 4, ALU.mult, ALU.add)
+        nc.vector.tensor_scalar(gain2_t[:], gain_t[:], -2.0, None, ALU.mult)
+
+        def gather_words(a, half):
+            cols = slice(half * HALF, (half + 1) * HALF)
+            entries = offs_t[:, half * HALF // 16 : (half + 1) * HALF // 16]
+            nc.vector.tensor_copy(out=v_w[a][:, cols], in_=tab_w[a][:].bitcast(U32).indirect(entries))
+
+        def cast_w1(a, b, scalar_m):
+            grouped = slot(a if b == 0 else PASSES - 1, [P, PACK * KP], BF16, f"grouped{a}{b}")
+            dst = grouped[:].rearrange("p (t m j) -> p m j t", t=PACK, j=PACK)
+            src = w1_raw[a, b][:].rearrange("p j (m t) -> p m j t", t=PACK)
+            if scalar_m > 0:
+                nc.scalar.copy(out=dst[:, :scalar_m], in_=src[:, :scalar_m])
+            if scalar_m < P:
+                nc.vector.tensor_copy(out=dst[:, scalar_m:], in_=src[:, scalar_m:])
+            return grouped
+
+        def quant_w1(a, b, grouped, parts):
+            width = KP // parts
+            for i in range(parts):
+                cols = slice(i * width, (i + 1) * width)
+                nc.vector.quantize_mx(
+                    out=w1_w[a, b][:, cols].bitcast(FP8X4),
+                    scales=w1_s[a, b][:, cols],
+                    in_=grouped[:, PACK * i * width : PACK * (i + 1) * width],
+                )
+
+        nc.vector.tensor_copy(out=v_s[:], in_=tab_s[:].indirect(offs_t[:]))
+        v_w[0] = keep.tile([P, S], U32, name="v_w0", align_bytes=64)
+        for a in range(PASSES):
+            if a > 0:
+                v_w[a] = slot(a - 1, [P, S], U32, f"v_w{a}")
+            gather_words(a, 0)
+            gather_words(a, 1)
+            last = a == PASSES - 1
+            grouped = cast_w1(a, 0, SPLIT_M if last else P)
+            quant_w1(a, 0, grouped, 2 if last else 1)
+            if not last:
+                load_w1(a + 1, 1)
+        tab2_w = staged([P, T2], I32, "tab2_w")
+        nc.sync.dma_start(out=tab2_w[:], in_=tab2_words[0].rearrange("p t i -> p (t i)").bitcast(I32))
+        late = {}
+
+        def stage1(b, c0, width):
+            cols = slice(c0, c0 + width)
+            sines = ring.tile([P, PACK, HALF], F32, name="sines", bufs=2, align_bytes=64)
+            for t in range(PACK):
+                acc = psum.tile([P, HALF], F32, name="acc", bufs=5)
+                for a in range(PASSES):
+                    nc.tensor.matmul_mx(
+                        out=acc[:, :width],
+                        lhsT=w1_w[a, b][:, t * P : (t + 1) * P].bitcast(FP8X4),
+                        lhsT_scale=w1_s[a, b][:, t * P : (t + 1) * P],
+                        rhs=v_w[a][:, cols].bitcast(FP8X4),
+                        rhs_scale=v_s[4 * a :, cols],
+                        start=(a == 0),
+                        stop=(a == PASSES - 1),
+                    )
+                nc.scalar.activation(
+                    out=sines[:, t, :width], in_=acc[:, :width], func=ACT.Sin,
+                    bias=bias_t[:, b, t : t + 1], scale=-0.5,
+                )
+            return sines
+
+        def square(sines, j0, step):
+            squares = ring.tile([P, PACK * 256], F32, name="squares", bufs=3, align_bytes=64)
+            nc.scalar.activation(
+                out=squares[:, : PACK * step].rearrange("p (c i t) -> p c t i", i=4, t=PACK),
+                in_=sines[:, :, j0 : j0 + step].rearrange("p t (c i) -> p c t i", i=4),
+                func=ACT.Square,
+            )
+            return squares
+
+        def finish_h(b, squares, c0, step):
+            h_bf = ring.tile([P, PACK * 256], BF16, name="h_bf", bufs=3, align_bytes=64)
+            nc.vector.scalar_tensor_tensor(
+                out=h_bf[:, : PACK * step].rearrange("p (j t) -> p j t", t=PACK),
+                in0=squares[:, : PACK * step].rearrange("p (j t) -> p j t", t=PACK),
+                scalar=0.5,
+                in1=gain2_t[:, b, :].unsqueeze(1).to_broadcast([P, step, PACK]),
+                op0=ALU.subtract,
+                op1=ALU.mult,
+            )
+            return h_bf
+
+        def quant_h(b, h_bf, c0, step):
+            cols = slice(c0, c0 + step)
+            nc.vector.quantize_mx(out=h_w[b][:, cols].bitcast(FP8X4), scales=h_s[b][:, cols], in_=h_bf[:, : PACK * step])
+
+        def stage2(c0, width):
+            cols = slice(c0, c0 + width)
+            for n in range(NT):
+                yacc = psum.tile([P, HALF], F32, name="yacc", bufs=3)
+                for b in range(BLOCKS):
+                    nc.tensor.matmul_mx(
+                        out=yacc[:, :width],
+                        lhsT=w2_w[:, b, 2 * n * P : 2 * (n + 1) * P].bitcast(FP4X4),
+                        lhsT_scale=w2_s[:, b, n * P : (n + 1) * P],
+                        rhs=h_w[b][:, cols].bitcast(FP8X4),
+                        rhs_scale=h_s[b][:, cols],
+                        start=(b == 0),
+                        stop=(b == BLOCKS - 1),
+                    )
+                nc.scalar.copy(out=y_t[n][:, cols], in_=yacc[:, :width])
+
+        def prepare_w1(a):
+            quant_w1(a, 1, cast_w1(a, 1, 0), 1)
+            if a == 0:
+                late["w3_raw"] = staged([P, PACK, N], F32, "w3_raw")
+                nc.sync.dma_start(out=late["w3_raw"][:], in_=w3.rearrange("(p j) c -> p j c", j=PACK))
+
+        def prepare_v2():
+            nc.vector.tensor_copy(out=v2_w[:], in_=tab2_w[:].bitcast(U32).indirect(offs2_t[:]))
+            late["v2_s"] = staged([P, PICK], U8, "v2_s")
+            nc.vector.tensor_copy(out=late["v2_s"][:], in_=tab2_s[:].indirect(offs2_t[:]))
+
+        def prepare_w3():
+            w3_raw = late["w3_raw"]
+            w3_bf = slot(PASSES - 1, [P, PACK * N], BF16, "w3_bf")
+            nc.vector.tensor_copy(
+                out=w3_bf[:].rearrange("p (c i j) -> p c j i", i=4, j=PACK),
+                in_=w3_raw[:].rearrange("p j (c i) -> p c j i", i=4),
+            )
+            nc.vector.quantize_mx(out=w3_w[:].bitcast(FP8X4), scales=w3_s[:], in_=w3_bf[:])
+
+        extras = {
+            0: [lambda: prepare_w1(0), lambda: prepare_w1(1)],
+            1: [lambda: prepare_w1(2)],
+            2: [prepare_v2, prepare_w3],
+        }
+        b_acc = []
+        pending = None
+        for k, (b, c0, width, step) in enumerate(CHUNKS):
+            sines = stage1(b, c0, width)
+            if pending is not None:
+                stage2(*pending)
+                pending = None
+            if k == len(CHUNKS) - 1:
+                for n in range(NT):
+                    acc = psum.tile([P, HALF], F32, name="acc", bufs=5)
+                    nc.tensor.matmul_mx(
+                        out=acc[:],
+                        lhsT=w3_w[:, n * P : (n + 1) * P].bitcast(FP8X4),
+                        lhsT_scale=w3_s[:, n * P : (n + 1) * P],
+                        rhs=v2_w[:].bitcast(FP8X4),
+                        rhs_scale=late["v2_s"][:],
+                        start=True,
+                        stop=True,
+                    )
+                    b_acc.append(acc)
+            todo = list(extras.get(k, []))
+            for j0 in range(0, width, step):
+                squares = square(sines, j0, step)
+                if todo:
+                    todo.pop(0)()
+                h_bf = finish_h(b, squares, c0 + j0, step)
+                quant_h(b, h_bf, c0 + j0, step)
+            if b == BLOCKS - 1:
+                pending = (c0, width)
+        stage2(*pending)
+
+        picked = [keep.tile([P, PICK], F32, name=f"picked{n}", align_bytes=64) for n in range(NT)]
+        product = [keep.tile([P, PICK], F32, name=f"product{n}", align_bytes=64) for n in range(NT)]
+        larger = {}
+
+        def pick(n):
+            nc.vector.tensor_copy(out=picked[n][:], in_=y_t[n][:].indirect(pos_t[:]))
+
+        def multiply(n):
+            nc.vector.tensor_tensor(out=product[n][:], in0=picked[n][:], in1=b_acc[n][:], op=ALU.mult)
+
+        def maximum(n):
+            larger[n] = ring.tile([P, PICK], F32, name="larger", bufs=2, align_bytes=64)
+            nc.vector.tensor_tensor(out=larger[n][:], in0=picked[n][:], in1=b_acc[n][:], op=ALU.max)
+
+        def add_store(n):
+            nc.vector.tensor_tensor(out=product[n][:], in0=product[n][:], in1=larger[n][:], op=ALU.add)
+            nc.sync.dma_start(out=out[n * P : (n + 1) * P, :], in_=product[n][:])
+
+        pick(0)
+        pick(1)
+        multiply(0)
+        maximum(0)
+        pick(2)
+        add_store(0)
+        multiply(1)
+        maximum(1)
+        multiply(2)
+        add_store(1)
+        maximum(2)
+        add_store(2)

@@ -24,7 +24,7 @@ PASSES = K // KP
 BLOCKS = H // KP
 NT = N // P
 HALF = 512
-CHUNKS = [(0, 0, 512, 256), (0, 512, 512, 256), (1, 0, 512, 256), (1, 512, 256, 256), (1, 768, 256, 128)]
+CHUNKS = [(0, 0, 512, 512), (0, 512, 512, 512), (1, 0, 512, 512), (1, 512, 256, 256), (1, 768, 256, 128)]
 SPLIT_M = 48
 
 
@@ -42,12 +42,10 @@ def tile_list_site_restocking_score_kernel(
         offs2_t = keep.tile([P, PICK // 16], U16, name="offs2_t")
         pos_t = keep.tile([P, PICK // 16], U16, name="pos_t")
 
-        tab_w = [keep.tile([P, T], I32, name=f"tab_w{a}", align_bytes=64) for a in range(PASSES)]
+        tab_w = [ring.tile([P, T], I32, name=f"tab_w{a}", tag=f"tab{a}", bufs=1, align_bytes=64) for a in range(PASSES)]
         tab_s = keep.tile([P, T], U8, name="tab_s", align_bytes=64)
         v_w = {}
-        v_s = keep.tile([P, S], U8, name="v_s", align_bytes=64)
-        tab2_s = keep.tile([P, T2], U8, name="tab2_s", align_bytes=64)
-        v2_w = keep.tile([P, PICK], U32, name="v2_w", align_bytes=64)
+        tab2_s = ring.tile([P, T2], U8, name="tab2_s", tag="slot2", bufs=1, align_bytes=64)
         w2_w = keep.tile([P, BLOCKS, 2 * N], U8, name="w2_w", align_bytes=64)
         w2_s = keep.tile([P, BLOCKS, N], U8, name="w2_s", align_bytes=64)
 
@@ -64,10 +62,9 @@ def tile_list_site_restocking_score_kernel(
         gain2_t = keep.tile([P, BLOCKS, PACK], F32, name="gain2_t")
         h_w = [keep.tile([P, S], U32, name=f"h_w{b}", align_bytes=64) for b in range(BLOCKS)]
         h_s = [keep.tile([P, S], U8, name=f"h_s{b}", align_bytes=64) for b in range(BLOCKS)]
-        y_t = [keep.tile([P, S], F32, name=f"y_t{n}", align_bytes=64) for n in range(NT)]
 
         def staged(shape, dtype, name):
-            return ring.tile(shape, dtype, name=name, tag="staged", bufs=4, align_bytes=64)
+            return keep.tile(shape, dtype, name=name, align_bytes=64)
 
         def slot(i, shape, dtype, name):
             return ring.tile(shape, dtype, name=name, tag=f"slot{i}", bufs=1, align_bytes=64)
@@ -83,22 +80,34 @@ def tile_list_site_restocking_score_kernel(
         nc.vector.memset(tab_s[:].bitcast(I32), 0)
         nc.vector.memset(tab2_s[:].bitcast(I32), 0)
         nc.vector.memset(w2_s[:].bitcast(I32), 0)
+        nc.scalar.dma_start(out=phase_t[:], in_=phase.rearrange("(b p t) -> p b t", p=P, t=PACK))
+        nc.scalar.dma_start(out=gain_t[:], in_=gain.rearrange("(b p t) -> p b t", p=P, t=PACK))
+        nc.sync.dma_start(out=offs_t[:], in_=offs)
         load_tab(0)
+        load_w1(0, 0)
+        load_tab(1)
+        load_w1(1, 0)
+        load_tab(2)
+        halves = []
+        for i in range(2):
+            half_raw = staged([P, PACK, KP // 2], F32, f"half_raw{i}")
+            rows = w1[(PASSES - 1) * KP :, i * KP // 2 : (i + 1) * KP // 2]
+            nc.sync.dma_start(out=half_raw[:], in_=rows.rearrange("(p j) c -> p j c", j=PACK))
+            halves.append(half_raw)
+        nc.sync.dma_start(out=offs2_t[:], in_=offs2)
+        for a in range(PASSES):
+            load_w1(a, 1)
+        w3_raw = staged([P, PACK, N], F32, "w3_raw")
+        nc.sync.dma_start(out=w3_raw[:], in_=w3.rearrange("(p j) c -> p j c", j=PACK))
+        nc.sync.dma_start(out=w2_w[:].bitcast(I32), in_=w2_words.rearrange("a p c -> p a c").bitcast(I32))
+        tab2_w = staged([P, T2], I32, "tab2_w")
+        nc.sync.dma_start(out=tab2_w[:], in_=tab2_words[0].rearrange("p t i -> p (t i)").bitcast(I32))
+        nc.sync.dma_start(out=pos_t[:], in_=pos1)
         for q in range(4):
-            nc.sync.dma_start(
+            nc.gpsimd.dma_start(
                 out=tab_s[32 * q : 32 * q + 4 * PASSES, :].bitcast(I32),
                 in_=tab_scales[:, 4 * q : 4 * q + 4, :].bitcast(I32),
             )
-        nc.sync.dma_start(out=offs_t[:], in_=offs)
-        nc.sync.dma_start(out=phase_t[:], in_=phase.rearrange("(b p t) -> p b t", p=P, t=PACK))
-        nc.sync.dma_start(out=gain_t[:], in_=gain.rearrange("(b p t) -> p b t", p=P, t=PACK))
-        nc.sync.dma_start(out=offs2_t[:], in_=offs2)
-        nc.sync.dma_start(out=pos_t[:], in_=pos1)
-        nc.sync.dma_start(out=w2_w[:].bitcast(I32), in_=w2_words.rearrange("a p c -> p a c").bitcast(I32))
-        load_w1(0, 0)
-        for a in range(1, PASSES):
-            load_tab(a)
-            load_w1(a, 0)
         for q in range(4):
             nc.gpsimd.dma_start(
                 out=tab2_s[32 * q : 32 * q + 4, :].bitcast(I32),
@@ -109,7 +118,6 @@ def tile_list_site_restocking_score_kernel(
                 out=w2_s[32 * q : 32 * q + 4, :, :].bitcast(I32),
                 in_=w2_scales[:, 4 * q : 4 * q + 4, :].rearrange("a r n -> r a n").bitcast(I32),
             )
-        load_w1(0, 1)
 
         nc.vector.tensor_scalar(bias_t[:], phase_t[:], -0.5, math.pi / 4, ALU.mult, ALU.add)
         nc.vector.tensor_scalar(gain2_t[:], gain_t[:], -2.0, None, ALU.mult)
@@ -139,27 +147,33 @@ def tile_list_site_restocking_score_kernel(
                     in_=grouped[:, PACK * i * width : PACK * (i + 1) * width],
                 )
 
-        nc.vector.tensor_copy(out=v_s[:], in_=tab_s[:].indirect(offs_t[:]))
         v_w[0] = keep.tile([P, S], U32, name="v_w0", align_bytes=64)
         for a in range(PASSES):
             if a > 0:
                 v_w[a] = slot(a - 1, [P, S], U32, f"v_w{a}")
             gather_words(a, 0)
             gather_words(a, 1)
-            last = a == PASSES - 1
-            grouped = cast_w1(a, 0, SPLIT_M if last else P)
-            quant_w1(a, 0, grouped, 2 if last else 1)
-            if not last:
-                load_w1(a + 1, 1)
-        tab2_w = staged([P, T2], I32, "tab2_w")
-        nc.sync.dma_start(out=tab2_w[:], in_=tab2_words[0].rearrange("p t i -> p (t i)").bitcast(I32))
-        late = {}
+            if a == 0:
+                v_s = ring.tile([P, S], U8, name="v_s", tag="tab0", bufs=1, align_bytes=64)
+                nc.vector.tensor_copy(out=v_s[:], in_=tab_s[:].indirect(offs_t[:]))
+            if a < PASSES - 1:
+                quant_w1(a, 0, cast_w1(a, 0, P), 1)
+        grouped = slot(PASSES, [P, PACK * KP], BF16, "grouped_last")
+        dst = grouped[:].rearrange("p (t m j) -> p m j t", t=PACK, j=PACK)
+        nc.scalar.copy(out=dst[:, : P // 2], in_=halves[0][:].rearrange("p j (m t) -> p m j t", t=PACK))
+        nc.vector.tensor_copy(out=dst[:, P // 2 :], in_=halves[1][:].rearrange("p j (m t) -> p m j t", t=PACK))
+        quant_w1(PASSES - 1, 0, grouped, 2)
+        v2_s = slot(PASSES, [P, PICK], U8, "v2_s")
+        nc.vector.tensor_copy(out=v2_s[:], in_=tab2_s[:].indirect(offs2_t[:]))
 
         def stage1(b, c0, width):
             cols = slice(c0, c0 + width)
-            sines = ring.tile([P, PACK, HALF], F32, name="sines", bufs=2, align_bytes=64)
+            if b == BLOCKS - 1 and c0 + width == S:
+                sines = ring.tile([P, PACK, width], F32, name="sines_last", tag="scores", bufs=1, align_bytes=64)
+            else:
+                sines = ring.tile([P, PACK, HALF], F32, name="sines", bufs=2, align_bytes=64)
             for t in range(PACK):
-                acc = psum.tile([P, HALF], F32, name="acc", bufs=5)
+                acc = psum.tile([P, HALF], F32, name="acc", bufs=8)
                 for a in range(PASSES):
                     nc.tensor.matmul_mx(
                         out=acc[:, :width],
@@ -177,7 +191,7 @@ def tile_list_site_restocking_score_kernel(
             return sines
 
         def square(sines, j0, step):
-            squares = ring.tile([P, PACK * 256], F32, name="squares", bufs=3, align_bytes=64)
+            squares = ring.tile([P, PACK * HALF], F32, name="squares", bufs=3, align_bytes=64)
             nc.scalar.activation(
                 out=squares[:, : PACK * step].rearrange("p (c i t) -> p c t i", i=4, t=PACK),
                 in_=sines[:, :, j0 : j0 + step].rearrange("p t (c i) -> p c t i", i=4),
@@ -186,7 +200,12 @@ def tile_list_site_restocking_score_kernel(
             return squares
 
         def finish_h(b, squares, c0, step):
-            h_bf = ring.tile([P, PACK * 256], BF16, name="h_bf", bufs=3, align_bytes=64)
+            if b == BLOCKS - 1 and c0 + step == S:
+                h_bf = ring.tile([P, PACK * step], BF16, name="h_bf_last", tag="last", bufs=1, align_bytes=64)
+            elif b == 0 and c0 == 0:
+                h_bf = slot(PASSES - 1, [P, PACK * HALF], BF16, "h_bf_first")
+            else:
+                h_bf = ring.tile([P, PACK * HALF], BF16, name="h_bf", bufs=2, align_bytes=64)
             nc.vector.scalar_tensor_tensor(
                 out=h_bf[:, : PACK * step].rearrange("p (j t) -> p j t", t=PACK),
                 in0=squares[:, : PACK * step].rearrange("p (j t) -> p j t", t=PACK),
@@ -201,35 +220,26 @@ def tile_list_site_restocking_score_kernel(
             cols = slice(c0, c0 + step)
             nc.vector.quantize_mx(out=h_w[b][:, cols].bitcast(FP8X4), scales=h_s[b][:, cols], in_=h_bf[:, : PACK * step])
 
-        def stage2(c0, width):
-            cols = slice(c0, c0 + width)
+        def stage2(y_all, c0, ranges):
             for n in range(NT):
-                yacc = psum.tile([P, HALF], F32, name="yacc", bufs=3)
-                for b in range(BLOCKS):
+                acc = psum.tile([P, HALF], F32, name="acc", bufs=8)
+                passes = [(0, c0, HALF)] + [(1, r0, width) for r0, width in ranges]
+                for i, (b, r0, width) in enumerate(passes):
                     nc.tensor.matmul_mx(
-                        out=yacc[:, :width],
+                        out=acc[:, r0 - c0 : r0 - c0 + width],
                         lhsT=w2_w[:, b, 2 * n * P : 2 * (n + 1) * P].bitcast(FP4X4),
                         lhsT_scale=w2_s[:, b, n * P : (n + 1) * P],
-                        rhs=h_w[b][:, cols].bitcast(FP8X4),
-                        rhs_scale=h_s[b][:, cols],
-                        start=(b == 0),
-                        stop=(b == BLOCKS - 1),
+                        rhs=h_w[b][:, r0 : r0 + width].bitcast(FP8X4),
+                        rhs_scale=h_s[b][:, r0 : r0 + width],
+                        start=(i == 0),
+                        stop=(i == len(passes) - 1),
                     )
-                nc.scalar.copy(out=y_t[n][:, cols], in_=yacc[:, :width])
+                nc.scalar.copy(out=y_all[:, n, c0 : c0 + HALF], in_=acc[:])
 
         def prepare_w1(a):
             quant_w1(a, 1, cast_w1(a, 1, 0), 1)
-            if a == 0:
-                late["w3_raw"] = staged([P, PACK, N], F32, "w3_raw")
-                nc.sync.dma_start(out=late["w3_raw"][:], in_=w3.rearrange("(p j) c -> p j c", j=PACK))
-
-        def prepare_v2():
-            nc.vector.tensor_copy(out=v2_w[:], in_=tab2_w[:].bitcast(U32).indirect(offs2_t[:]))
-            late["v2_s"] = staged([P, PICK], U8, "v2_s")
-            nc.vector.tensor_copy(out=late["v2_s"][:], in_=tab2_s[:].indirect(offs2_t[:]))
 
         def prepare_w3():
-            w3_raw = late["w3_raw"]
             w3_bf = slot(PASSES - 1, [P, PACK * N], BF16, "w3_bf")
             nc.vector.tensor_copy(
                 out=w3_bf[:].rearrange("p (c i j) -> p c j i", i=4, j=PACK),
@@ -237,48 +247,41 @@ def tile_list_site_restocking_score_kernel(
             )
             nc.vector.quantize_mx(out=w3_w[:].bitcast(FP8X4), scales=w3_s[:], in_=w3_bf[:])
 
-        extras = {
-            0: [lambda: prepare_w1(0), lambda: prepare_w1(1)],
-            1: [lambda: prepare_w1(2)],
-            2: [prepare_v2, prepare_w3],
-        }
+        for a in range(PASSES):
+            prepare_w1(a)
         b_acc = []
-        pending = None
         for k, (b, c0, width, step) in enumerate(CHUNKS):
             sines = stage1(b, c0, width)
-            if pending is not None:
-                stage2(*pending)
-                pending = None
-            if k == len(CHUNKS) - 1:
-                for n in range(NT):
-                    acc = psum.tile([P, HALF], F32, name="acc", bufs=5)
-                    nc.tensor.matmul_mx(
-                        out=acc[:],
-                        lhsT=w3_w[:, n * P : (n + 1) * P].bitcast(FP8X4),
-                        lhsT_scale=w3_s[:, n * P : (n + 1) * P],
-                        rhs=v2_w[:].bitcast(FP8X4),
-                        rhs_scale=late["v2_s"][:],
-                        start=True,
-                        stop=True,
-                    )
-                    b_acc.append(acc)
-            todo = list(extras.get(k, []))
             for j0 in range(0, width, step):
                 squares = square(sines, j0, step)
-                if todo:
-                    todo.pop(0)()
                 h_bf = finish_h(b, squares, c0 + j0, step)
                 quant_h(b, h_bf, c0 + j0, step)
-            if b == BLOCKS - 1:
-                pending = (c0, width)
-        stage2(*pending)
+            if k == 1:
+                prepare_w3()
+        y_all = ring.tile([P, NT, S], F32, name="y_all", tag="scores", bufs=1, align_bytes=64)
+        stage2(y_all, 0, [(0, 512)])
+        stage2(y_all, HALF, [(512, 256), (768, 128), (896, 128)])
+        v2_w = ring.tile([P, PICK], U32, name="v2_w", tag="last", bufs=1, align_bytes=64)
+        nc.vector.tensor_copy(out=v2_w[:], in_=tab2_w[:].bitcast(U32).indirect(offs2_t[:]))
+        for n in range(NT):
+            acc = psum.tile([P, HALF], F32, name="acc", bufs=8)
+            nc.tensor.matmul_mx(
+                out=acc[:],
+                lhsT=w3_w[:, n * P : (n + 1) * P].bitcast(FP8X4),
+                lhsT_scale=w3_s[:, n * P : (n + 1) * P],
+                rhs=v2_w[:].bitcast(FP8X4),
+                rhs_scale=v2_s[:],
+                start=True,
+                stop=True,
+            )
+            b_acc.append(acc)
 
         picked = [keep.tile([P, PICK], F32, name=f"picked{n}", align_bytes=64) for n in range(NT)]
         product = [keep.tile([P, PICK], F32, name=f"product{n}", align_bytes=64) for n in range(NT)]
         larger = {}
 
         def pick(n):
-            nc.vector.tensor_copy(out=picked[n][:], in_=y_t[n][:].indirect(pos_t[:]))
+            nc.vector.tensor_copy(out=picked[n][:], in_=y_all[:, n, :].indirect(pos_t[:]))
 
         def multiply(n):
             nc.vector.tensor_tensor(out=product[n][:], in0=picked[n][:], in1=b_acc[n][:], op=ALU.mult)
@@ -288,8 +291,11 @@ def tile_list_site_restocking_score_kernel(
             nc.vector.tensor_tensor(out=larger[n][:], in0=picked[n][:], in1=b_acc[n][:], op=ALU.max)
 
         def add_store(n):
-            nc.vector.tensor_tensor(out=product[n][:], in0=product[n][:], in1=larger[n][:], op=ALU.add)
-            nc.sync.dma_start(out=out[n * P : (n + 1) * P, :], in_=product[n][:])
+            parts = 2 if n == NT - 1 else 1
+            for i in range(parts):
+                cols = slice(i * PICK // parts, (i + 1) * PICK // parts)
+                nc.vector.tensor_tensor(out=product[n][:, cols], in0=product[n][:, cols], in1=larger[n][:, cols], op=ALU.add)
+                nc.sync.dma_start(out=out[n * P : (n + 1) * P, cols], in_=product[n][:, cols])
 
         pick(0)
         pick(1)

@@ -73,7 +73,7 @@ def tile_list_site_restocking_score_kernel(
             nc.sync.dma_start(out=tab_w[a][:], in_=tab_words[a].rearrange("p t i -> p (t i)").bitcast(I32))
 
         def load_w1(a, b):
-            w1_raw[a, b] = staged([P, PACK, KP], F32, f"w1_raw{a}{b}")
+            w1_raw[a, b] = ring.tile([P, PACK, KP], F32, name=f"w1_raw{a}{b}", tag=f"raw{a}{b}", bufs=1, align_bytes=64)
             rows = w1[a * KP : (a + 1) * KP, b * KP : (b + 1) * KP]
             nc.sync.dma_start(out=w1_raw[a, b][:], in_=rows.rearrange("(p j) c -> p j c", j=PACK))
 
@@ -128,7 +128,8 @@ def tile_list_site_restocking_score_kernel(
             nc.vector.tensor_copy(out=v_w[a][:, cols], in_=tab_w[a][:].bitcast(U32).indirect(entries))
 
         def cast_w1(a, b, scalar_m):
-            grouped = slot(a if b == 0 else PASSES - 1, [P, PACK * KP], BF16, f"grouped{a}{b}")
+            tag = f"slot{a}" if b == 0 else ("slot2" if a == 0 else f"raw{a - 1}1")
+            grouped = ring.tile([P, PACK * KP], BF16, name=f"grouped{a}{b}", tag=tag, bufs=1, align_bytes=64)
             dst = grouped[:].rearrange("p (t m j) -> p m j t", t=PACK, j=PACK)
             src = w1_raw[a, b][:].rearrange("p j (m t) -> p m j t", t=PACK)
             if scalar_m > 0:
@@ -203,7 +204,7 @@ def tile_list_site_restocking_score_kernel(
             if b == BLOCKS - 1 and c0 + step == S:
                 h_bf = ring.tile([P, PACK * step], BF16, name="h_bf_last", tag="last", bufs=1, align_bytes=64)
             elif b == 0 and c0 == 0:
-                h_bf = slot(PASSES - 1, [P, PACK * HALF], BF16, "h_bf_first")
+                h_bf = ring.tile([P, PACK * HALF], BF16, name="h_bf_first", tag="raw11", bufs=1, align_bytes=64)
             else:
                 h_bf = ring.tile([P, PACK * HALF], BF16, name="h_bf", bufs=2, align_bytes=64)
             nc.vector.scalar_tensor_tensor(
@@ -240,7 +241,7 @@ def tile_list_site_restocking_score_kernel(
             quant_w1(a, 1, cast_w1(a, 1, 0), 1)
 
         def prepare_w3():
-            w3_bf = slot(PASSES - 1, [P, PACK * N], BF16, "w3_bf")
+            w3_bf = ring.tile([P, PACK * N], BF16, name="w3_bf", tag="raw11", bufs=1, align_bytes=64)
             nc.vector.tensor_copy(
                 out=w3_bf[:].rearrange("p (c i j) -> p c j i", i=4, j=PACK),
                 in_=w3_raw[:].rearrange("p j (c i) -> p c j i", i=4),
@@ -294,7 +295,8 @@ def tile_list_site_restocking_score_kernel(
             parts = 2 if n == NT - 1 else 1
             for i in range(parts):
                 cols = slice(i * PICK // parts, (i + 1) * PICK // parts)
-                nc.vector.tensor_tensor(out=product[n][:, cols], in0=product[n][:, cols], in1=larger[n][:, cols], op=ALU.add)
+                engine = nc.vector if n == NT - 1 else nc.gpsimd
+                engine.tensor_tensor(out=product[n][:, cols], in0=product[n][:, cols], in1=larger[n][:, cols], op=ALU.add)
                 nc.sync.dma_start(out=out[n * P : (n + 1) * P, cols], in_=product[n][:, cols])
 
         pick(0)

import math
from contextlib import ExitStack

import concourse.mybir as mybir

K, T, S, H, N, K2, T2, PICK = 1536, 4096, 1024, 1024, 384, 512, 1024, 512
FLOPS = 2 * K * H * S + 2 * H * N * S + 2 * K2 * N * PICK

F32 = mybir.dt.float32
BF16 = mybir.dt.bfloat16
I32 = mybir.dt.int32
U32 = mybir.dt.uint32
U16 = mybir.dt.uint16
U8 = mybir.dt.uint8
FP8X4 = mybir.dt.float8_e4m3fn_x4
FP4X4 = mybir.dt.float4_e2m1fn_x4
ACT = mybir.ActivationFunctionType
ALU = mybir.AluOpType

P = 128
PACK = 4
KP = P * PACK
PASSES = K // KP
BLOCKS = H // KP
NT = N // P
HALF = 512
CHUNKS = [(0, 0, 512, 512), (0, 512, 512, 512), (1, 0, 512, 512), (1, 512, 256, 256), (1, 768, 256, 128)]
SPLIT_M = 48


def tile_list_site_restocking_score_kernel(
    tc, tab_words, tab_scales, tab2_words, tab2_scales, offs, offs2, pos1,
    w1, phase, gain, w2_words, w2_scales, w3, out,
):
    nc = tc.nc
    with ExitStack() as ctx:
        keep = ctx.enter_context(tc.tile_pool(name="keep", bufs=1))
        ring = ctx.enter_context(tc.tile_pool(name="ring", bufs=2))
        psum = ctx.enter_context(tc.psum_pool(name="psum", bufs=1))

        offs_t = keep.tile([P, S // 16], U16, name="offs_t")
        offs2_t = keep.tile([P, PICK // 16], U16, name="offs2_t")
        pos_t = keep.tile([P, PICK // 16], U16, name="pos_t")

        tab_w = [ring.tile([P, T], I32, name=f"tab_w{a}", tag=f"tab{a}", bufs=1, align_bytes=64) for a in range(PASSES)]
        tab_s = keep.tile([P, T], U8, name="tab_s", align_bytes=64)
        v_w = {}
        tab2_s = ring.tile([P, T2], U8, name="tab2_s", tag="slot2", bufs=1, align_bytes=64)
        w2_w = keep.tile([P, BLOCKS, 2 * N], U8, name="w2_w", align_bytes=64)
        w2_s = keep.tile([P, BLOCKS, N], U8, name="w2_s", align_bytes=64)

        w1_raw, w1_w, w1_s = {}, {}, {}
        for b in range(BLOCKS):
            for a in range(PASSES):
                w1_w[a, b] = keep.tile([P, KP], U32, name=f"w1_w{a}{b}", align_bytes=64)
                w1_s[a, b] = keep.tile([P, KP], U8, name=f"w1_s{a}{b}", align_bytes=64)
        w3_w = keep.tile([P, N], U32, name="w3_w", align_bytes=64)
        w3_s = keep.tile([P, N], U8, name="w3_s", align_bytes=64)
        phase_t = keep.tile([P, BLOCKS, PACK], F32, name="phase_t")
        gain_t = keep.tile([P, BLOCKS, PACK], F32, name="gain_t")
        bias_t = keep.tile([P, BLOCKS, PACK], F32, name="bias_t")
        gain2_t = keep.tile([P, BLOCKS, PACK], F32, name="gain2_t")
        h_w = [keep.tile([P, S], U32, name=f"h_w{b}", align_bytes=64) for b in range(BLOCKS)]
        h_s = [keep.tile([P, S], U8, name=f"h_s{b}", align_bytes=64) for b in range(BLOCKS)]

        def staged(shape, dtype, name):
            return keep.tile(shape, dtype, name=name, align_bytes=64)

        def slot(i, shape, dtype, name):
            return ring.tile(shape, dtype, name=name, tag=f"slot{i}", bufs=1, align_bytes=64)

        def load_tab(a):
            nc.sync.dma_start(out=tab_w[a][:], in_=tab_words[a].rearrange("p t i -> p (t i)").bitcast(I32))

        def load_w1(a, b):
            w1_raw[a, b] = ring.tile([P, PACK, KP], F32, name=f"w1_raw{a}{b}", tag=f"raw{a}{b}", bufs=1, align_bytes=64)
            rows = w1[a * KP : (a + 1) * KP, b * KP : (b + 1) * KP]
            nc.sync.dma_start(out=w1_raw[a, b][:], in_=rows.rearrange("(p j) c -> p j c", j=PACK))

        nc.vector.memset(tab_s[:].bitcast(I32), 0)
        nc.vector.memset(tab2_s[:].bitcast(I32), 0)
        nc.vector.memset(w2_s[:].bitcast(I32), 0)
        nc.scalar.dma_start(out=phase_t[:], in_=phase.rearrange("(b p t) -> p b t", p=P, t=PACK))
        nc.scalar.dma_start(out=gain_t[:], in_=gain.rearrange("(b p t) -> p b t", p=P, t=PACK))
        nc.sync.dma_start(out=offs_t[:], in_=offs)
        load_tab(0)
        load_w1(0, 0)
        load_tab(1)
        load_w1(1, 0)
        load_tab(2)
        halves = []
        for i in range(2):
            half_raw = staged([P, PACK, KP // 2], F32, f"half_raw{i}")
            rows = w1[(PASSES - 1) * KP :, i * KP // 2 : (i + 1) * KP // 2]
            nc.sync.dma_start(out=half_raw[:], in_=rows.rearrange("(p j) c -> p j c", j=PACK))
            halves.append(half_raw)
        nc.sync.dma_start(out=offs2_t[:], in_=offs2)
        for a in range(PASSES):
            load_w1(a, 1)
        w3_raw = staged([P, PACK, N], F32, "w3_raw")
        nc.sync.dma_start(out=w3_raw[:], in_=w3.rearrange("(p j) c -> p j c", j=PACK))
        nc.sync.dma_start(out=w2_w[:].bitcast(I32), in_=w2_words.rearrange("a p c -> p a c").bitcast(I32))
        tab2_w = staged([P, T2], I32, "tab2_w")
        nc.sync.dma_start(out=tab2_w[:], in_=tab2_words[0].rearrange("p t i -> p (t i)").bitcast(I32))
        nc.sync.dma_start(out=pos_t[:], in_=pos1)
        for q in range(4):
            nc.gpsimd.dma_start(
                out=tab_s[32 * q : 32 * q + 4 * PASSES, :].bitcast(I32),
                in_=tab_scales[:, 4 * q : 4 * q + 4, :].bitcast(I32),
            )
        for q in range(4):
            nc.gpsimd.dma_start(
                out=tab2_s[32 * q : 32 * q + 4, :].bitcast(I32),
                in_=tab2_scales[0, 4 * q : 4 * q + 4, :].bitcast(I32),
            )
        for q in range(4):
            nc.gpsimd.dma_start(
                out=w2_s[32 * q : 32 * q + 4, :, :].bitcast(I32),
                in_=w2_scales[:, 4 * q : 4 * q + 4, :].rearrange("a r n -> r a n").bitcast(I32),
            )

        nc.vector.tensor_scalar(bias_t[:], phase_t[:], -0.5, math.pi / 4, ALU.mult, ALU.add)
        nc.vector.tensor_scalar(gain2_t[:], gain_t[:], -2.0, None, ALU.mult)

        def gather_words(a, half):
            cols = slice(half * HALF, (half + 1) * HALF)
            entries = offs_t[:, half * HALF // 16 : (half + 1) * HALF // 16]
            nc.vector.tensor_copy(out=v_w[a][:, cols], in_=tab_w[a][:].bitcast(U32).indirect(entries))

        def cast_w1(a, b, scalar_m):
            tag = f"slot{a}" if b == 0 else ("slot2" if a == 0 else f"raw{a - 1}1")
            grouped = ring.tile([P, PACK * KP], BF16, name=f"grouped{a}{b}", tag=tag, bufs=1, align_bytes=64)
            dst = grouped[:].rearrange("p (t m j) -> p m j t", t=PACK, j=PACK)
            src = w1_raw[a, b][:].rearrange("p j (m t) -> p m j t", t=PACK)
            if scalar_m > 0:
                nc.scalar.copy(out=dst[:, :scalar_m], in_=src[:, :scalar_m])
            if scalar_m < P:
                nc.vector.tensor_copy(out=dst[:, scalar_m:], in_=src[:, scalar_m:])
            return grouped

        def quant_w1(a, b, grouped, parts):
            width = KP // parts
            for i in range(parts):
                cols = slice(i * width, (i + 1) * width)
                nc.vector.quantize_mx(
                    out=w1_w[a, b][:, cols].bitcast(FP8X4),
                    scales=w1_s[a, b][:, cols],
                    in_=grouped[:, PACK * i * width : PACK * (i + 1) * width],
                )

        v_w[0] = keep.tile([P, S], U32, name="v_w0", align_bytes=64)
        for a in range(PASSES):
            if a > 0:
                v_w[a] = slot(a - 1, [P, S], U32, f"v_w{a}")
            gather_words(a, 0)
            gather_words(a, 1)
            if a == 0:
                v_s = ring.tile([P, S], U8, name="v_s", tag="tab0", bufs=1, align_bytes=64)
                nc.vector.tensor_copy(out=v_s[:], in_=tab_s[:].indirect(offs_t[:]))
            if a < PASSES - 1:
                quant_w1(a, 0, cast_w1(a, 0, P), 1)
        grouped = slot(PASSES, [P, PACK * KP], BF16, "grouped_last")
        dst = grouped[:].rearrange("p (t m j) -> p m j t", t=PACK, j=PACK)
        nc.scalar.copy(out=dst[:, : P // 2], in_=halves[0][:].rearrange("p j (m t) -> p m j t", t=PACK))
        nc.vector.tensor_copy(out=dst[:, P // 2 :], in_=halves[1][:].rearrange("p j (m t) -> p m j t", t=PACK))
        quant_w1(PASSES - 1, 0, grouped, 2)
        v2_s = slot(PASSES, [P, PICK], U8, "v2_s")
        nc.vector.tensor_copy(out=v2_s[:], in_=tab2_s[:].indirect(offs2_t[:]))

        def stage1(b, c0, width):
            cols = slice(c0, c0 + width)
            if b == BLOCKS - 1 and c0 + width == S:
                sines = ring.tile([P, PACK, width], F32, name="sines_last", tag="scores", bufs=1, align_bytes=64)
            else:
                sines = ring.tile([P, PACK, HALF], F32, name="sines", bufs=2, align_bytes=64)
            for t in range(PACK):
                acc = psum.tile([P, HALF], F32, name="acc", bufs=8)
                for a in range(PASSES):
                    nc.tensor.matmul_mx(
                        out=acc[:, :width],
                        lhsT=w1_w[a, b][:, t * P : (t + 1) * P].bitcast(FP8X4),
                        lhsT_scale=w1_s[a, b][:, t * P : (t + 1) * P],
                        rhs=v_w[a][:, cols].bitcast(FP8X4),
                        rhs_scale=v_s[4 * a :, cols],
                        start=(a == 0),
                        stop=(a == PASSES - 1),
                    )
                nc.scalar.activation(
                    out=sines[:, t, :width], in_=acc[:, :width], func=ACT.Sin,
                    bias=bias_t[:, b, t : t + 1], scale=-0.5,
                )
            return sines

        def square(sines, j0, step):
            squares = ring.tile([P, PACK * HALF], F32, name="squares", bufs=3, align_bytes=64)
            nc.scalar.activation(
                out=squares[:, : PACK * step].rearrange("p (c i t) -> p c t i", i=4, t=PACK),
                in_=sines[:, :, j0 : j0 + step].rearrange("p t (c i) -> p c t i", i=4),
                func=ACT.Square,
            )
            return squares

        def finish_h(b, squares, c0, step):
            if b == BLOCKS - 1 and c0 + step == S:
                h_bf = ring.tile([P, PACK * step], BF16, name="h_bf_last", tag="last", bufs=1, align_bytes=64)
            elif b == 0 and c0 == 0:
                h_bf = ring.tile([P, PACK * HALF], BF16, name="h_bf_first", tag="raw11", bufs=1, align_bytes=64)
            else:
                h_bf = ring.tile([P, PACK * HALF], BF16, name="h_bf", bufs=2, align_bytes=64)
            nc.vector.scalar_tensor_tensor(
                out=h_bf[:, : PACK * step].rearrange("p (j t) -> p j t", t=PACK),
                in0=squares[:, : PACK * step].rearrange("p (j t) -> p j t", t=PACK),
                scalar=0.5,
                in1=gain2_t[:, b, :].unsqueeze(1).to_broadcast([P, step, PACK]),
                op0=ALU.subtract,
                op1=ALU.mult,
            )
            return h_bf

        def quant_h(b, h_bf, c0, step):
            cols = slice(c0, c0 + step)
            nc.vector.quantize_mx(out=h_w[b][:, cols].bitcast(FP8X4), scales=h_s[b][:, cols], in_=h_bf[:, : PACK * step])

        def stage2(y_all, c0, ranges):
            for n in range(NT):
                acc = psum.tile([P, HALF], F32, name="acc", bufs=8)
                passes = [(0, c0, HALF)] + [(1, r0, width) for r0, width in ranges]
                for i, (b, r0, width) in enumerate(passes):
                    nc.tensor.matmul_mx(
                        out=acc[:, r0 - c0 : r0 - c0 + width],
                        lhsT=w2_w[:, b, 2 * n * P : 2 * (n + 1) * P].bitcast(FP4X4),
                        lhsT_scale=w2_s[:, b, n * P : (n + 1) * P],
                        rhs=h_w[b][:, r0 : r0 + width].bitcast(FP8X4),
                        rhs_scale=h_s[b][:, r0 : r0 + width],
                        start=(i == 0),
                        stop=(i == len(passes) - 1),
                    )
                nc.scalar.copy(out=y_all[:, n, c0 : c0 + HALF], in_=acc[:])

        def prepare_w1(a):
            quant_w1(a, 1, cast_w1(a, 1, 0), 1)

        def prepare_w3():
            w3_bf = ring.tile([P, PACK * N], BF16, name="w3_bf", tag="raw11", bufs=1, align_bytes=64)
            nc.vector.tensor_copy(
                out=w3_bf[:].rearrange("p (c i j) -> p c j i", i=4, j=PACK),
                in_=w3_raw[:].rearrange("p j (c i) -> p c j i", i=4),
            )
            nc.vector.quantize_mx(out=w3_w[:].bitcast(FP8X4), scales=w3_s[:], in_=w3_bf[:])

        for a in range(PASSES):
            prepare_w1(a)
        b_acc = []
        for k, (b, c0, width, step) in enumerate(CHUNKS):
            sines = stage1(b, c0, width)
            for j0 in range(0, width, step):
                squares = square(sines, j0, step)
                h_bf = finish_h(b, squares, c0 + j0, step)
                quant_h(b, h_bf, c0 + j0, step)
            if k == 1:
                prepare_w3()
        y_all = ring.tile([P, NT, S], F32, name="y_all", tag="scores", bufs=1, align_bytes=64)
        stage2(y_all, 0, [(0, 512)])
        stage2(y_all, HALF, [(512, 256), (768, 128), (896, 128)])
        v2_w = ring.tile([P, PICK], U32, name="v2_w", tag="last", bufs=1, align_bytes=64)
        nc.vector.tensor_copy(out=v2_w[:], in_=tab2_w[:].bitcast(U32).indirect(offs2_t[:]))
        for n in range(NT):
            acc = psum.tile([P, HALF], F32, name="acc", bufs=8)
            nc.tensor.matmul_mx(
                out=acc[:],
                lhsT=w3_w[:, n * P : (n + 1) * P].bitcast(FP8X4),
                lhsT_scale=w3_s[:, n * P : (n + 1) * P],
                rhs=v2_w[:].bitcast(FP8X4),
                rhs_scale=v2_s[:],
                start=True,
                stop=True,
            )
            b_acc.append(acc)

        picked = [keep.tile([P, PICK], F32, name=f"picked{n}", align_bytes=64) for n in range(NT)]
        product = [keep.tile([P, PICK], F32, name=f"product{n}", align_bytes=64) for n in range(NT)]
        larger = {}

        def pick(n):
            nc.vector.tensor_copy(out=picked[n][:], in_=y_all[:, n, :].indirect(pos_t[:]))

        def multiply(n):
            nc.vector.tensor_tensor(out=product[n][:], in0=picked[n][:], in1=b_acc[n][:], op=ALU.mult)

        def maximum(n):
            larger[n] = ring.tile([P, PICK], F32, name="larger", bufs=2, align_bytes=64)
            nc.vector.tensor_tensor(out=larger[n][:], in0=picked[n][:], in1=b_acc[n][:], op=ALU.max)

        def add_store(n):
            parts = 2 if n == NT - 1 else 1
            for i in range(parts):
                cols = slice(i * PICK // parts, (i + 1) * PICK // parts)
                engine = nc.vector if n == NT - 1 else nc.gpsimd
                engine.tensor_tensor(out=product[n][:, cols], in0=product[n][:, cols], in1=larger[n][:, cols], op=ALU.add)
                nc.sync.dma_start(out=out[n * P : (n + 1) * P, cols], in_=product[n][:, cols])

        pick(0)
        pick(1)
        multiply(0)
        maximum(0)
        pick(2)
        add_store(0)
        multiply(1)
        maximum(1)
        multiply(2)
        add_store(1)
        maximum(2)
        add_store(2)
